import numpy as np
import ml_dtypes


def mxq(x, axis, fmt="e4m3"):
    dtype, down = {"e4m3": (ml_dtypes.float8_e4m3fn, 7), "e5m2": (ml_dtypes.float8_e5m2, 14)}[fmt]
    v = np.moveaxis(np.asarray(x, np.float32).astype(ml_dtypes.bfloat16).astype(np.float64), axis, -1)
    blocks = v.reshape(v.shape[:-1] + (-1, 32))
    amax = np.abs(blocks).max(-1, keepdims=True)
    byte = np.maximum(np.where(amax > 0, np.frexp(amax)[1] - 1 + 127, 0) - down, 1)
    scale = np.exp2(byte - 127.0)
    codes = (blocks / scale).astype(np.float32).astype(dtype).astype(np.float64)
    return np.moveaxis((codes * scale).reshape(v.shape), -1, axis)


WIDE = False


def mx_kscale(k):
    if not WIDE:
        return np.ones(k)
    levels = np.array([10, -10, 5, -5, 0])
    if k % 512:
        return np.exp2(np.random.permutation(np.resize(levels, k // 32))).repeat(32)
    a = np.empty((k // 512, 16))
    for p in range(k // 512):
        a[p, :8] = np.random.permutation(np.resize(levels, 8))
        for g in range(8):
            far = levels[np.abs(levels - a[p, g]) >= 10]
            a[p, g + 8] = far[np.random.randint(len(far))]
    return np.exp2(a.ravel()).repeat(32)


def f64(x):
    return np.asarray(x).astype(np.float64)


def striped(idx):
    return np.tile(np.asarray(idx).reshape(-1, 16).T, (8, 1)).astype(np.uint16)


def unstriped(offs):
    return offs[:16].T.reshape(-1).astype(np.int64)

def sigmoid(v):
    return 1.0 / (1.0 + np.exp(-v))


B, N, T, D, NQ = 1, 512, 2048, 512, 256
DV = 512


def setup_inputs():
    n = np.random.standard_normal
    idx = np.random.permutation(T)[:B * N]
    u = mx_kscale(N)
    ut = np.ones(T)
    ut[idx] = u
    return {
        "vT": (n((DV, T)) / ut).astype(np.float32),
        "wT": (np.random.dirichlet(np.ones(N), NQ).T[None] * u[:, None] * 16).astype(np.float32),
        "og": (n((B, NQ, DV))).astype(np.float32),
        "offs": striped(idx),
    }


def reference(vT, wT, og, offs):
    idx = unstriped(offs)
    pick = lambda x, which: x[:, which].reshape(x.shape[0], B, -1).transpose(1, 0, 2)
    wq = mxq(f64(wT), 1, "e4m3")
    o = wq.transpose(0, 2, 1) @ mxq(pick(f64(vT), idx).transpose(0, 2, 1), 1, "e4m3")
    r_ = o * sigmoid(f64(og))
    return r_

@@ -1,0 +1,114 @@
+from contextlib import ExitStack
+
+import concourse.mybir as mybir
+from concourse.masks import make_identity
+
+N, T, NQ, DV = 512, 2048, 256, 512
+FLOPS = 2 * N * NQ * DV
+
+F32 = mybir.dt.float32
+BF16 = mybir.dt.bfloat16
+U32 = mybir.dt.uint32
+U16 = mybir.dt.uint16
+U8 = mybir.dt.uint8
+FP8X4 = mybir.dt.float8_e4m3fn_x4
+SIGMOID = mybir.ActivationFunctionType.Sigmoid
+MULT = mybir.AluOpType.mult
+
+P = 128
+PACK = 4
+E_TILES = DV // P
+Q_TILES = NQ // P
+EARLY = DV - P
+
+
+def tile_attend_wsum_gate_f_topk_kernel(tc, vT, wT, og, offs, out):
+    nc = tc.nc
+    with ExitStack() as ctx:
+        sb = ctx.enter_context(tc.tile_pool(name="sb", bufs=1))
+        psum = ctx.enter_context(tc.psum_pool(name="psum", bufs=1))
+
+        offsets = sb.tile([P, N // 16], U16, name="offsets")
+        pool_tiles = [sb.tile([P, T], F32, name=f"pool{j}") for j in range(E_TILES)]
+        w_raw = sb.tile([P, PACK, NQ], F32, name="w_raw")
+        gate_raw = [sb.tile([P, DV], F32, name=f"gate_raw{i}") for i in range(Q_TILES)]
+
+        nc.sync.dma_start(out=pool_tiles[0][:], in_=vT[0:P, :])
+        nc.sync.dma_start(offsets[:], offs)
+        nc.sync.dma_start(out=w_raw[:], in_=wT[0].rearrange("(p t) q -> p t q", t=PACK))
+        for j in range(1, E_TILES):
+            nc.sync.dma_start(out=pool_tiles[j][:], in_=vT[j * P : (j + 1) * P, :])
+        for i in range(Q_TILES):
+            nc.sync.dma_start(out=gate_raw[i][:], in_=og[0, i * P : (i + 1) * P, :])
+
+        identity = sb.tile([P, P], F32, name="identity")
+        make_identity(nc, identity[:])
+
+        w_grouped = sb.tile([P, NQ, PACK], BF16, name="w_grouped", align_bytes=64)
+        w_codes = sb.tile([P, NQ], U32, name="w_codes", align_bytes=64)
+        w_scales = sb.tile([P, NQ], U8, name="w_scales", align_bytes=64)
+
+        acc_early = [psum.tile([P, EARLY], F32, name=f"acc_early{i}") for i in range(Q_TILES)]
+        acc_last = psum.tile([P, Q_TILES, P], F32, name="acc_last")
+
+        def quantize_weights():
+            nc.vector.tensor_copy(out=w_grouped[:], in_=w_raw[:].rearrange("p t q -> p q t"))
+            nc.vector.quantize_mx(
+                out=w_codes[:].bitcast(FP8X4),
+                scales=w_scales[:],
+                in_=w_grouped[:].rearrange("p q t -> p (q t)"),
+            )
+
+        def gather_and_turn(j):
+            picked = sb.tile([P, N], BF16, name=f"picked{j}", align_bytes=64)
+            nc.vector.tensor_copy(picked[:], pool_tiles[j][:].indirect(offsets[:]))
+            words = picked[:].bitcast(F32)
+            turned = psum.tile([P, 2, P], F32, name=f"turned{j}")
+            for u in range(2):
+                nc.tensor.transpose(turned[:, u, :], words[:, u::2], identity[:])
+            return turned
+
+        def quantize_and_multiply(j, turned, copy):
+            grouped = sb.tile([P, P * PACK], BF16, name=f"grouped{j}", align_bytes=64)
+            copy(
+                out=grouped[:].bitcast(F32).rearrange("p (e u) -> p e u", u=2),
+                in_=turned[:].rearrange("p u e -> p e u"),
+            )
+            v_codes = sb.tile([P, P], U32, name=f"v_codes{j}", align_bytes=64)
+            v_scales = sb.tile([P, P], U8, name=f"v_scales{j}", align_bytes=64)
+            nc.vector.quantize_mx(out=v_codes[:].bitcast(FP8X4), scales=v_scales[:], in_=grouped[:])
+            for i in range(Q_TILES):
+                q_cols = slice(i * P, (i + 1) * P)
+                acc = acc_last[:, i, :] if j == E_TILES - 1 else acc_early[i][:, j * P : (j + 1) * P]
+                nc.tensor.matmul_mx(
+                    out=acc,
+                    lhsT=w_codes[:, q_cols].bitcast(FP8X4),
+                    lhsT_scale=w_scales[:, q_cols],
+                    rhs=v_codes[:].bitcast(FP8X4),
+                    rhs_scale=v_scales[:],
+                    start=True,
+                    stop=True,
+                )
+
+        for j in range(E_TILES - 1):
+            turned = gather_and_turn(j)
+            if j == 0:
+                quantize_weights()
+            quantize_and_multiply(j, turned, nc.vector.tensor_copy)
+
+        turned_last = gather_and_turn(E_TILES - 1)
+
+        for i in range(Q_TILES):
+            gate = sb.tile([P, EARLY], F32, name=f"gate{i}")
+            nc.scalar.activation(gate[:], gate_raw[i][:, :EARLY], SIGMOID)
+            result = sb.tile([P, EARLY], F32, name=f"result{i}")
+            nc.vector.tensor_tensor(result[:], acc_early[i][:], gate[:], MULT)
+            nc.sync.dma_start(out=out[0, i * P : (i + 1) * P, :EARLY], in_=result[:])
+
+        quantize_and_multiply(E_TILES - 1, turned_last, nc.scalar.copy)
+        gate_last = sb.tile([P, Q_TILES, P], F32, name="gate_last")
+        for i in range(Q_TILES):
+            nc.scalar.activation(gate_last[:, i, :], gate_raw[i][:, EARLY:], SIGMOID)
+        result_last = sb.tile([P, Q_TILES, P], F32, name="result_last")
+        nc.vector.tensor_tensor(result_last[:], acc_last[:], gate_last[:], MULT)
+        nc.sync.dma_start(out=out[0, :, EARLY:].rearrange("(i p) e -> p i e", p=P), in_=result_last[:])

@@ -20,6 +20,9 @@ PACK = 4
 E_TILES = DV // P
 Q_TILES = NQ // P
 EARLY = DV - P
+HALF = DV // 2
+GATE_HEAD = 16
+SHARE = 64
 
 
 def tile_attend_wsum_gate_f_topk_kernel(tc, vT, wT, og, offs, out):
@@ -31,84 +34,111 @@ def tile_attend_wsum_gate_f_topk_kernel(tc, vT, wT, og, offs, out):
         offsets = sb.tile([P, N // 16], U16, name="offsets")
         pool_tiles = [sb.tile([P, T], F32, name=f"pool{j}") for j in range(E_TILES)]
         w_raw = sb.tile([P, PACK, NQ], F32, name="w_raw")
-        gate_raw = [sb.tile([P, DV], F32, name=f"gate_raw{i}") for i in range(Q_TILES)]
+        gate_raw = [sb.tile([P, DV], F32, name=f"gate_raw{i}", align_bytes=64) for i in range(Q_TILES)]
+        gate = sb.tile([P, Q_TILES, DV], F32, name="gate")
 
         nc.sync.dma_start(out=pool_tiles[0][:], in_=vT[0:P, :])
         nc.sync.dma_start(offsets[:], offs)
-        nc.sync.dma_start(out=w_raw[:], in_=wT[0].rearrange("(p t) q -> p t q", t=PACK))
+        nc.sync.dma_start(out=gate_raw[0][:, :GATE_HEAD], in_=og[0, :P, :GATE_HEAD])
         for j in range(1, E_TILES):
             nc.sync.dma_start(out=pool_tiles[j][:], in_=vT[j * P : (j + 1) * P, :])
-        for i in range(Q_TILES):
-            nc.sync.dma_start(out=gate_raw[i][:], in_=og[0, i * P : (i + 1) * P, :])
+        nc.sync.dma_start(out=w_raw[:], in_=wT[0].rearrange("(p t) q -> p t q", t=PACK))
+        nc.sync.dma_start(out=gate_raw[0][:, GATE_HEAD:], in_=og[0, :P, GATE_HEAD:])
+        nc.sync.dma_start(out=gate_raw[1][:], in_=og[0, P:, :])
 
         identity = sb.tile([P, P], F32, name="identity")
         make_identity(nc, identity[:])
+        nc.scalar.activation(gate[:, 0, :GATE_HEAD], gate_raw[0][:, :GATE_HEAD], SIGMOID)
 
-        w_grouped = sb.tile([P, NQ, PACK], BF16, name="w_grouped", align_bytes=64)
-        w_codes = sb.tile([P, NQ], U32, name="w_codes", align_bytes=64)
-        w_scales = sb.tile([P, NQ], U8, name="w_scales", align_bytes=64)
+        def operand(name, columns, tag=None):
+            grouped = sb.tile([P, columns * PACK], BF16, name=f"{name}_grouped", tag=tag or f"{name}_grouped", align_bytes=64)
+            codes = sb.tile([P, columns], U32, name=f"{name}_codes", align_bytes=64)
+            scales = sb.tile([P, columns], U8, name=f"{name}_scales", align_bytes=64)
+            return grouped, codes, scales
 
-        acc_early = [psum.tile([P, EARLY], F32, name=f"acc_early{i}") for i in range(Q_TILES)]
-        acc_last = psum.tile([P, Q_TILES, P], F32, name="acc_last")
-
-        def quantize_weights():
-            nc.vector.tensor_copy(out=w_grouped[:], in_=w_raw[:].rearrange("p t q -> p q t"))
-            nc.vector.quantize_mx(
-                out=w_codes[:].bitcast(FP8X4),
-                scales=w_scales[:],
-                in_=w_grouped[:].rearrange("p q t -> p (q t)"),
-            )
+        def quantize(op):
+            grouped, codes, scales = op
+            nc.vector.quantize_mx(out=codes[:].bitcast(FP8X4), scales=scales[:], in_=grouped[:])
 
         def gather_and_turn(j):
             picked = sb.tile([P, N], BF16, name=f"picked{j}", align_bytes=64)
-            nc.vector.tensor_copy(picked[:], pool_tiles[j][:].indirect(offsets[:]))
+            nc.vector.tensor_copy(
+                picked[:].rearrange("e (u p h) -> e p u h", u=2, h=2), pool_tiles[j][:].indirect(offsets[:])
+            )
             words = picked[:].bitcast(F32)
             turned = psum.tile([P, 2, P], F32, name=f"turned{j}")
             for u in range(2):
-                nc.tensor.transpose(turned[:, u, :], words[:, u::2], identity[:])
+                nc.tensor.transpose(turned[:, u, :], words[:, u * P : (u + 1) * P], identity[:])
             return turned
 
-        def quantize_and_multiply(j, turned, copy):
-            grouped = sb.tile([P, P * PACK], BF16, name=f"grouped{j}", align_bytes=64)
-            copy(
-                out=grouped[:].bitcast(F32).rearrange("p (e u) -> p e u", u=2),
+        def copy_out(turned, op, c0):
+            nc.scalar.copy(
+                out=op[0][:, c0 * PACK : (c0 + P) * PACK].bitcast(F32).rearrange("p (e u) -> p e u", u=2),
                 in_=turned[:].rearrange("p u e -> p e u"),
             )
-            v_codes = sb.tile([P, P], U32, name=f"v_codes{j}", align_bytes=64)
-            v_scales = sb.tile([P, P], U8, name=f"v_scales{j}", align_bytes=64)
-            nc.vector.quantize_mx(out=v_codes[:].bitcast(FP8X4), scales=v_scales[:], in_=grouped[:])
-            for i in range(Q_TILES):
-                q_cols = slice(i * P, (i + 1) * P)
-                acc = acc_last[:, i, :] if j == E_TILES - 1 else acc_early[i][:, j * P : (j + 1) * P]
-                nc.tensor.matmul_mx(
-                    out=acc,
-                    lhsT=w_codes[:, q_cols].bitcast(FP8X4),
-                    lhsT_scale=w_scales[:, q_cols],
-                    rhs=v_codes[:].bitcast(FP8X4),
-                    rhs_scale=v_scales[:],
-                    start=True,
-                    stop=True,
-                )
 
-        for j in range(E_TILES - 1):
-            turned = gather_and_turn(j)
-            if j == 0:
-                quantize_weights()
-            quantize_and_multiply(j, turned, nc.vector.tensor_copy)
+        def group_weights(copy, q0, width, op, c0):
+            copy(
+                out=op[0][:, c0 * PACK : (c0 + width) * PACK].rearrange("p (c r t) -> p c t r", r=4, t=PACK),
+                in_=w_raw[:, :, q0 : q0 + width].rearrange("p t (c r) -> p c t r", r=4),
+            )
 
-        turned_last = gather_and_turn(E_TILES - 1)
+        def multiply(acc, w_op, w0, v_op, v0, width):
+            nc.tensor.matmul_mx(
+                out=acc,
+                lhsT=w_op[1][:, w0 : w0 + P].bitcast(FP8X4),
+                lhsT_scale=w_op[2][:, w0 : w0 + P],
+                rhs=v_op[1][:, v0 : v0 + width].bitcast(FP8X4),
+                rhs_scale=v_op[2][:, v0 : v0 + width],
+                start=True,
+                stop=True,
+            )
 
-        for i in range(Q_TILES):
-            gate = sb.tile([P, EARLY], F32, name=f"gate{i}")
-            nc.scalar.activation(gate[:], gate_raw[i][:, :EARLY], SIGMOID)
-            result = sb.tile([P, EARLY], F32, name=f"result{i}")
-            nc.vector.tensor_tensor(result[:], acc_early[i][:], gate[:], MULT)
-            nc.sync.dma_start(out=out[0, i * P : (i + 1) * P, :EARLY], in_=result[:])
+        first = operand("first", 2 * P)
+        mixed = operand("mixed", 2 * P)
+        w_first = operand("w_first", P)
+        weights = [(w_first, 0), (mixed, P)]
 
-        quantize_and_multiply(E_TILES - 1, turned_last, nc.scalar.copy)
-        gate_last = sb.tile([P, Q_TILES, P], F32, name="gate_last")
-        for i in range(Q_TILES):
-            nc.scalar.activation(gate_last[:, i, :], gate_raw[i][:, EARLY:], SIGMOID)
-        result_last = sb.tile([P, Q_TILES, P], F32, name="result_last")
-        nc.vector.tensor_tensor(result_last[:], acc_last[:], gate_last[:], MULT)
-        nc.sync.dma_start(out=out[0, :, EARLY:].rearrange("(i p) e -> p i e", p=P), in_=result_last[:])
+        copy_out(gather_and_turn(0), first, 0)
+        copy_out(gather_and_turn(1), first, P)
+        quantize(first)
+        copy_out(gather_and_turn(2), mixed, 0)
+        turned_last = gather_and_turn(3)
+
+        group_weights(nc.vector.tensor_copy, 0, P, w_first, 0)
+        group_weights(nc.vector.tensor_copy, P, SHARE, mixed, P)
+        group_weights(nc.scalar.copy, P + SHARE, P - SHARE, mixed, P + SHARE)
+        quantize(w_first)
+        quantize(mixed)
+
+        acc_first = [psum.tile([P, HALF], F32, name=f"acc_first{i}") for i in range(Q_TILES)]
+        acc_third = psum.tile([P, Q_TILES, P], F32, name="acc_third")
+        acc_last = psum.tile([P, Q_TILES, P], F32, name="acc_last")
+        for i, (w_op, w0) in enumerate(weights):
+            multiply(acc_first[i][:], w_op, w0, first, 0, HALF)
+        for i, (w_op, w0) in enumerate(weights):
+            multiply(acc_third[:, i, :], w_op, w0, mixed, 0, P)
+
+        def gate_and_store(name, acc, rows, cols):
+            result = sb.tile(list(acc.shape), F32, name=name)
+            nc.vector.tensor_tensor(result[:], acc, gate[:, rows, cols], MULT)
+            nc.sync.dma_start(out=out_tiles[:, rows, cols], in_=result[:])
+
+        out_tiles = out[0].rearrange("(i p) e -> p i e", p=P)
+        nc.scalar.activation(gate[:, 0, GATE_HEAD:HALF], gate_raw[0][:, GATE_HEAD:HALF], SIGMOID)
+        nc.scalar.activation(gate[:, 0, HALF:], gate_raw[0][:, HALF:], SIGMOID)
+        gate_and_store("result0", acc_first[0][:], 0, slice(0, HALF))
+        last = (
+            gate_raw[0][:, :HALF].bitcast(BF16),
+            sb.tile([P, P], U32, name="last_codes", align_bytes=64),
+            sb.tile([P, P], U8, name="last_scales", align_bytes=64),
+        )
+        copy_out(turned_last, last, 0)
+        nc.scalar.activation(gate[:, 1, :HALF], gate_raw[1][:, :HALF], SIGMOID)
+        nc.scalar.activation(gate[:, 1, HALF:], gate_raw[1][:, HALF:], SIGMOID)
+        quantize(last)
+        for i, (w_op, w0) in enumerate(weights):
+            multiply(acc_last[:, i, :], w_op, w0, last, 0, P)
+        gate_and_store("result1", acc_first[1][:], 1, slice(0, HALF))
+        gate_and_store("result2", acc_third[:], slice(0, Q_TILES), slice(HALF, EARLY))
+        gate_and_store("result3", acc_last[:], slice(0, Q_TILES), slice(EARLY, DV))

@@ -17,12 +17,13 @@ MULT = mybir.AluOpType.mult
 
 P = 128
 PACK = 4
+LIST_ROWS = 16
 E_TILES = DV // P
 Q_TILES = NQ // P
-EARLY = DV - P
 HALF = DV // 2
 GATE_HEAD = 16
-SHARE = 64
+VECTOR_SHARE = 64
+RUN = 4
 
 
 def tile_attend_wsum_gate_f_topk_kernel(tc, vT, wT, og, offs, out):
@@ -31,114 +32,109 @@ def tile_attend_wsum_gate_f_topk_kernel(tc, vT, wT, og, offs, out):
         sb = ctx.enter_context(tc.tile_pool(name="sb", bufs=1))
         psum = ctx.enter_context(tc.psum_pool(name="psum", bufs=1))
 
-        offsets = sb.tile([P, N // 16], U16, name="offsets")
+        offsets = sb.tile([P, N // LIST_ROWS], U16, name="offsets")
         pool_tiles = [sb.tile([P, T], F32, name=f"pool{j}") for j in range(E_TILES)]
         w_raw = sb.tile([P, PACK, NQ], F32, name="w_raw")
-        gate_raw = [sb.tile([P, DV], F32, name=f"gate_raw{i}", align_bytes=64) for i in range(Q_TILES)]
+        og_tiles = [sb.tile([P, DV], F32, name=f"og{i}", align_bytes=64) for i in range(Q_TILES)]
         gate = sb.tile([P, Q_TILES, DV], F32, name="gate")
 
         nc.sync.dma_start(out=pool_tiles[0][:], in_=vT[0:P, :])
         nc.sync.dma_start(offsets[:], offs)
-        nc.sync.dma_start(out=gate_raw[0][:, :GATE_HEAD], in_=og[0, :P, :GATE_HEAD])
+        nc.sync.dma_start(out=og_tiles[0][:, :GATE_HEAD], in_=og[0, :P, :GATE_HEAD])
         for j in range(1, E_TILES):
             nc.sync.dma_start(out=pool_tiles[j][:], in_=vT[j * P : (j + 1) * P, :])
         nc.sync.dma_start(out=w_raw[:], in_=wT[0].rearrange("(p t) q -> p t q", t=PACK))
-        nc.sync.dma_start(out=gate_raw[0][:, GATE_HEAD:], in_=og[0, :P, GATE_HEAD:])
-        nc.sync.dma_start(out=gate_raw[1][:], in_=og[0, P:, :])
+        nc.sync.dma_start(out=og_tiles[0][:, GATE_HEAD:], in_=og[0, :P, GATE_HEAD:])
+        nc.sync.dma_start(out=og_tiles[1][:], in_=og[0, P:, :])
+
+        def sigmoid_of_gate(i, c0, c1):
+            nc.scalar.activation(gate[:, i, c0:c1], og_tiles[i][:, c0:c1], SIGMOID)
 
         identity = sb.tile([P, P], F32, name="identity")
         make_identity(nc, identity[:])
-        nc.scalar.activation(gate[:, 0, :GATE_HEAD], gate_raw[0][:, :GATE_HEAD], SIGMOID)
+        sigmoid_of_gate(0, 0, GATE_HEAD)
 
-        def operand(name, columns, tag=None):
-            grouped = sb.tile([P, columns * PACK], BF16, name=f"{name}_grouped", tag=tag or f"{name}_grouped", align_bytes=64)
+        def grouped_tile(name, columns):
+            return sb.tile([P, columns * PACK], BF16, name=f"{name}_grouped", align_bytes=64)[:]
+
+        def mx_tiles(name, columns):
             codes = sb.tile([P, columns], U32, name=f"{name}_codes", align_bytes=64)
             scales = sb.tile([P, columns], U8, name=f"{name}_scales", align_bytes=64)
-            return grouped, codes, scales
+            return codes, scales
 
-        def quantize(op):
-            grouped, codes, scales = op
-            nc.vector.quantize_mx(out=codes[:].bitcast(FP8X4), scales=scales[:], in_=grouped[:])
+        def quantize(mx, grouped):
+            codes, scales = mx
+            nc.vector.quantize_mx(out=codes[:].bitcast(FP8X4), scales=scales[:], in_=grouped)
 
         def gather_and_turn(j):
             picked = sb.tile([P, N], BF16, name=f"picked{j}", align_bytes=64)
             nc.vector.tensor_copy(
                 picked[:].rearrange("e (u p h) -> e p u h", u=2, h=2), pool_tiles[j][:].indirect(offsets[:])
             )
-            words = picked[:].bitcast(F32)
+            pairs = picked[:].bitcast(F32)
             turned = psum.tile([P, 2, P], F32, name=f"turned{j}")
             for u in range(2):
-                nc.tensor.transpose(turned[:, u, :], words[:, u * P : (u + 1) * P], identity[:])
+                nc.tensor.transpose(turned[:, u, :], pairs[:, u * P : (u + 1) * P], identity[:])
             return turned
 
-        def copy_out(turned, op, c0):
+        def group_values(turned, grouped, c0):
             nc.scalar.copy(
-                out=op[0][:, c0 * PACK : (c0 + P) * PACK].bitcast(F32).rearrange("p (e u) -> p e u", u=2),
+                out=grouped[:, c0 * PACK : (c0 + P) * PACK].bitcast(F32).rearrange("p (e u) -> p e u", u=2),
                 in_=turned[:].rearrange("p u e -> p e u"),
             )
 
-        def group_weights(copy, q0, width, op, c0):
+        def group_weights(copy, q0, width, grouped, c0):
             copy(
-                out=op[0][:, c0 * PACK : (c0 + width) * PACK].rearrange("p (c r t) -> p c t r", r=4, t=PACK),
-                in_=w_raw[:, :, q0 : q0 + width].rearrange("p t (c r) -> p c t r", r=4),
+                out=grouped[:, c0 * PACK : (c0 + width) * PACK].rearrange("p (c r t) -> p c t r", r=RUN, t=PACK),
+                in_=w_raw[:, :, q0 : q0 + width].rearrange("p t (c r) -> p c t r", r=RUN),
             )
 
-        def multiply(acc, w_op, w0, v_op, v0, width):
+        def multiply(acc, w_mx, w0, v_mx, width):
             nc.tensor.matmul_mx(
                 out=acc,
-                lhsT=w_op[1][:, w0 : w0 + P].bitcast(FP8X4),
-                lhsT_scale=w_op[2][:, w0 : w0 + P],
-                rhs=v_op[1][:, v0 : v0 + width].bitcast(FP8X4),
-                rhs_scale=v_op[2][:, v0 : v0 + width],
+                lhsT=w_mx[0][:, w0 : w0 + P].bitcast(FP8X4),
+                lhsT_scale=w_mx[1][:, w0 : w0 + P],
+                rhs=v_mx[0][:, :width].bitcast(FP8X4),
+                rhs_scale=v_mx[1][:, :width],
                 start=True,
                 stop=True,
             )
 
-        first = operand("first", 2 * P)
-        mixed = operand("mixed", 2 * P)
-        w_first = operand("w_first", P)
-        weights = [(w_first, 0), (mixed, P)]
+        v01_grouped, v01 = grouped_tile("v01", 2 * P), mx_tiles("v01", 2 * P)
+        v2_w1_grouped, v2_w1 = grouped_tile("v2_w1", 2 * P), mx_tiles("v2_w1", 2 * P)
+        w0_grouped, w0_mx = grouped_tile("w0", P), mx_tiles("w0", P)
+        weights = [(w0_mx, 0), (v2_w1, P)]
 
-        copy_out(gather_and_turn(0), first, 0)
-        copy_out(gather_and_turn(1), first, P)
-        quantize(first)
-        copy_out(gather_and_turn(2), mixed, 0)
+        group_values(gather_and_turn(0), v01_grouped, 0)
+        group_values(gather_and_turn(1), v01_grouped, P)
+        quantize(v01, v01_grouped)
+        group_values(gather_and_turn(2), v2_w1_grouped, 0)
         turned_last = gather_and_turn(3)
 
-        group_weights(nc.vector.tensor_copy, 0, P, w_first, 0)
-        group_weights(nc.vector.tensor_copy, P, SHARE, mixed, P)
-        group_weights(nc.scalar.copy, P + SHARE, P - SHARE, mixed, P + SHARE)
-        quantize(w_first)
-        quantize(mixed)
+        group_weights(nc.vector.tensor_copy, 0, P, w0_grouped, 0)
+        group_weights(nc.vector.tensor_copy, P, VECTOR_SHARE, v2_w1_grouped, P)
+        group_weights(nc.scalar.copy, P + VECTOR_SHARE, P - VECTOR_SHARE, v2_w1_grouped, P + VECTOR_SHARE)
+        quantize(w0_mx, w0_grouped)
+        quantize(v2_w1, v2_w1_grouped)
 
-        acc_first = [psum.tile([P, HALF], F32, name=f"acc_first{i}") for i in range(Q_TILES)]
-        acc_third = psum.tile([P, Q_TILES, P], F32, name="acc_third")
-        acc_last = psum.tile([P, Q_TILES, P], F32, name="acc_last")
-        for i, (w_op, w0) in enumerate(weights):
-            multiply(acc_first[i][:], w_op, w0, first, 0, HALF)
-        for i, (w_op, w0) in enumerate(weights):
-            multiply(acc_third[:, i, :], w_op, w0, mixed, 0, P)
+        acc = [[psum.tile([P, HALF], F32, name=f"acc{i}{h}") for h in range(2)] for i in range(Q_TILES)]
+        for i, (w_mx, w0) in enumerate(weights):
+            multiply(acc[i][0][:], w_mx, w0, v01, HALF)
+        for i, (w_mx, w0) in enumerate(weights):
+            multiply(acc[i][1][:, :P], w_mx, w0, v2_w1, P)
 
-        def gate_and_store(name, acc, rows, cols):
-            result = sb.tile(list(acc.shape), F32, name=name)
-            nc.vector.tensor_tensor(result[:], acc, gate[:, rows, cols], MULT)
-            nc.sync.dma_start(out=out_tiles[:, rows, cols], in_=result[:])
+        sigmoid_of_gate(0, GATE_HEAD, HALF)
+        sigmoid_of_gate(0, HALF, DV)
+        v3_grouped, v3 = og_tiles[0][:, :HALF].bitcast(BF16), mx_tiles("v3", P)
+        group_values(turned_last, v3_grouped, 0)
+        sigmoid_of_gate(1, 0, HALF)
+        sigmoid_of_gate(1, HALF, DV)
+        quantize(v3, v3_grouped)
+        for i, (w_mx, w0) in enumerate(weights):
+            multiply(acc[i][1][:, P:], w_mx, w0, v3, P)
 
-        out_tiles = out[0].rearrange("(i p) e -> p i e", p=P)
-        nc.scalar.activation(gate[:, 0, GATE_HEAD:HALF], gate_raw[0][:, GATE_HEAD:HALF], SIGMOID)
-        nc.scalar.activation(gate[:, 0, HALF:], gate_raw[0][:, HALF:], SIGMOID)
-        gate_and_store("result0", acc_first[0][:], 0, slice(0, HALF))
-        last = (
-            gate_raw[0][:, :HALF].bitcast(BF16),
-            sb.tile([P, P], U32, name="last_codes", align_bytes=64),
-            sb.tile([P, P], U8, name="last_scales", align_bytes=64),
-        )
-        copy_out(turned_last, last, 0)
-        nc.scalar.activation(gate[:, 1, :HALF], gate_raw[1][:, :HALF], SIGMOID)
-        nc.scalar.activation(gate[:, 1, HALF:], gate_raw[1][:, HALF:], SIGMOID)
-        quantize(last)
-        for i, (w_op, w0) in enumerate(weights):
-            multiply(acc_last[:, i, :], w_op, w0, last, 0, P)
-        gate_and_store("result1", acc_first[1][:], 1, slice(0, HALF))
-        gate_and_store("result2", acc_third[:], slice(0, Q_TILES), slice(HALF, EARLY))
-        gate_and_store("result3", acc_last[:], slice(0, Q_TILES), slice(EARLY, DV))
+        for h in range(2):
+            cols = slice(h * HALF, (h + 1) * HALF)
+            for i in range(Q_TILES):
+                nc.vector.tensor_tensor(og_tiles[i][:, cols], acc[i][h][:], gate[:, i, cols], MULT)
+                nc.sync.dma_start(out=out[0, i * P : (i + 1) * P, cols], in_=og_tiles[i][:, cols])

@@ -33,14 +33,14 @@ def tile_attend_wsum_gate_f_topk_kernel(tc, vT, wT, og, offs, out):
         psum = ctx.enter_context(tc.psum_pool(name="psum", bufs=1))
 
         offsets = sb.tile([P, N // LIST_ROWS], U16, name="offsets")
-        pool_tiles = [sb.tile([P, T], F32, name=f"pool{j}") for j in range(E_TILES)]
+        pool_tiles = [sb.tile([P, T], F32, name=f"pool{j}", align_bytes=64) for j in range(E_TILES)]
         w_raw = sb.tile([P, PACK, NQ], F32, name="w_raw")
         og_tiles = [sb.tile([P, DV], F32, name=f"og{i}", align_bytes=64) for i in range(Q_TILES)]
         gate = sb.tile([P, Q_TILES, DV], F32, name="gate")
 
-        nc.sync.dma_start(out=pool_tiles[0][:], in_=vT[0:P, :])
+        nc.scalar.dma_start(out=pool_tiles[0][:], in_=vT[0:P, :])
         nc.sync.dma_start(offsets[:], offs)
-        nc.sync.dma_start(out=og_tiles[0][:, :GATE_HEAD], in_=og[0, :P, :GATE_HEAD])
+        nc.scalar.dma_start(out=og_tiles[0][:, :GATE_HEAD], in_=og[0, :P, :GATE_HEAD])
         for j in range(1, E_TILES):
             nc.sync.dma_start(out=pool_tiles[j][:], in_=vT[j * P : (j + 1) * P, :])
         nc.sync.dma_start(out=w_raw[:], in_=wT[0].rearrange("(p t) q -> p t q", t=PACK))
@@ -57,8 +57,8 @@ def tile_attend_wsum_gate_f_topk_kernel(tc, vT, wT, og, offs, out):
         def grouped_tile(name, columns):
             return sb.tile([P, columns * PACK], BF16, name=f"{name}_grouped", align_bytes=64)[:]
 
-        def mx_tiles(name, columns):
-            codes = sb.tile([P, columns], U32, name=f"{name}_codes", align_bytes=64)
+        def mx_tiles(name, columns, codes_tag=None):
+            codes = sb.tile([P, columns], U32, name=f"{name}_codes", tag=codes_tag or f"{name}_codes", align_bytes=64)
             scales = sb.tile([P, columns], U8, name=f"{name}_scales", align_bytes=64)
             return codes, scales
 
@@ -100,15 +100,16 @@ def tile_attend_wsum_gate_f_topk_kernel(tc, vT, wT, og, offs, out):
                 stop=True,
             )
 
-        v01_grouped, v01 = grouped_tile("v01", 2 * P), mx_tiles("v01", 2 * P)
+        v01_grouped = grouped_tile("v01", 2 * P)
         v2_w1_grouped, v2_w1 = grouped_tile("v2_w1", 2 * P), mx_tiles("v2_w1", 2 * P)
         w0_grouped, w0_mx = grouped_tile("w0", P), mx_tiles("w0", P)
         weights = [(w0_mx, 0), (v2_w1, P)]
 
         group_values(gather_and_turn(0), v01_grouped, 0)
         group_values(gather_and_turn(1), v01_grouped, P)
-        quantize(v01, v01_grouped)
         group_values(gather_and_turn(2), v2_w1_grouped, 0)
+        v01 = mx_tiles("v01", 2 * P, codes_tag="pool2")
+        quantize(v01, v01_grouped)
         turned_last = gather_and_turn(3)
 
         group_weights(nc.vector.tensor_copy, 0, P, w0_grouped, 0)

from contextlib import ExitStack

import concourse.mybir as mybir
from concourse.masks import make_identity

N, T, NQ, DV = 512, 2048, 256, 512
FLOPS = 2 * N * NQ * DV

F32 = mybir.dt.float32
BF16 = mybir.dt.bfloat16
U32 = mybir.dt.uint32
U16 = mybir.dt.uint16
U8 = mybir.dt.uint8
FP8X4 = mybir.dt.float8_e4m3fn_x4
SIGMOID = mybir.ActivationFunctionType.Sigmoid
MULT = mybir.AluOpType.mult

P = 128
PACK = 4
LIST_ROWS = 16
E_TILES = DV // P
Q_TILES = NQ // P
HALF = DV // 2
GATE_HEAD = 16
VECTOR_SHARE = 64
RUN = 4


def tile_attend_wsum_gate_f_topk_kernel(tc, vT, wT, og, offs, out):
    nc = tc.nc
    with ExitStack() as ctx:
        sb = ctx.enter_context(tc.tile_pool(name="sb", bufs=1))
        psum = ctx.enter_context(tc.psum_pool(name="psum", bufs=1))

        offsets = sb.tile([P, N // LIST_ROWS], U16, name="offsets")
        pool_tiles = [sb.tile([P, T], F32, name=f"pool{j}", align_bytes=64) for j in range(E_TILES)]
        w_raw = sb.tile([P, PACK, NQ], F32, name="w_raw")
        og_tiles = [sb.tile([P, DV], F32, name=f"og{i}", align_bytes=64) for i in range(Q_TILES)]
        gate = sb.tile([P, Q_TILES, DV], F32, name="gate")

        nc.scalar.dma_start(out=pool_tiles[0][:], in_=vT[0:P, :])
        nc.sync.dma_start(offsets[:], offs)
        nc.scalar.dma_start(out=og_tiles[0][:, :GATE_HEAD], in_=og[0, :P, :GATE_HEAD])
        for j in range(1, E_TILES):
            nc.sync.dma_start(out=pool_tiles[j][:], in_=vT[j * P : (j + 1) * P, :])
        nc.sync.dma_start(out=w_raw[:], in_=wT[0].rearrange("(p t) q -> p t q", t=PACK))
        nc.sync.dma_start(out=og_tiles[0][:, GATE_HEAD:], in_=og[0, :P, GATE_HEAD:])
        nc.sync.dma_start(out=og_tiles[1][:], in_=og[0, P:, :])

        def sigmoid_of_gate(i, c0, c1):
            nc.scalar.activation(gate[:, i, c0:c1], og_tiles[i][:, c0:c1], SIGMOID)

        identity = sb.tile([P, P], F32, name="identity")
        make_identity(nc, identity[:])
        sigmoid_of_gate(0, 0, GATE_HEAD)

        def grouped_tile(name, columns):
            return sb.tile([P, columns * PACK], BF16, name=f"{name}_grouped", align_bytes=64)[:]

        def mx_tiles(name, columns, codes_tag=None):
            codes = sb.tile([P, columns], U32, name=f"{name}_codes", tag=codes_tag or f"{name}_codes", align_bytes=64)
            scales = sb.tile([P, columns], U8, name=f"{name}_scales", align_bytes=64)
            return codes, scales

        def quantize(mx, grouped):
            codes, scales = mx
            nc.vector.quantize_mx(out=codes[:].bitcast(FP8X4), scales=scales[:], in_=grouped)

        def gather_and_turn(j):
            picked = sb.tile([P, N], BF16, name=f"picked{j}", align_bytes=64)
            nc.vector.tensor_copy(
                picked[:].rearrange("e (u p h) -> e p u h", u=2, h=2), pool_tiles[j][:].indirect(offsets[:])
            )
            pairs = picked[:].bitcast(F32)
            turned = psum.tile([P, 2, P], F32, name=f"turned{j}")
            for u in range(2):
                nc.tensor.transpose(turned[:, u, :], pairs[:, u * P : (u + 1) * P], identity[:])
            return turned

        def group_values(turned, grouped, c0):
            nc.scalar.copy(
                out=grouped[:, c0 * PACK : (c0 + P) * PACK].bitcast(F32).rearrange("p (e u) -> p e u", u=2),
                in_=turned[:].rearrange("p u e -> p e u"),
            )

        def group_weights(copy, q0, width, grouped, c0):
            copy(
                out=grouped[:, c0 * PACK : (c0 + width) * PACK].rearrange("p (c r t) -> p c t r", r=RUN, t=PACK),
                in_=w_raw[:, :, q0 : q0 + width].rearrange("p t (c r) -> p c t r", r=RUN),
            )

        def multiply(acc, w_mx, w0, v_mx, width):
            nc.tensor.matmul_mx(
                out=acc,
                lhsT=w_mx[0][:, w0 : w0 + P].bitcast(FP8X4),
                lhsT_scale=w_mx[1][:, w0 : w0 + P],
                rhs=v_mx[0][:, :width].bitcast(FP8X4),
                rhs_scale=v_mx[1][:, :width],
                start=True,
                stop=True,
            )

        v01_grouped = grouped_tile("v01", 2 * P)
        v2_w1_grouped, v2_w1 = grouped_tile("v2_w1", 2 * P), mx_tiles("v2_w1", 2 * P)
        w0_grouped, w0_mx = grouped_tile("w0", P), mx_tiles("w0", P)
        weights = [(w0_mx, 0), (v2_w1, P)]

        group_values(gather_and_turn(0), v01_grouped, 0)
        group_values(gather_and_turn(1), v01_grouped, P)
        group_values(gather_and_turn(2), v2_w1_grouped, 0)
        v01 = mx_tiles("v01", 2 * P, codes_tag="pool2")
        quantize(v01, v01_grouped)
        turned_last = gather_and_turn(3)

        group_weights(nc.vector.tensor_copy, 0, P, w0_grouped, 0)
        group_weights(nc.vector.tensor_copy, P, VECTOR_SHARE, v2_w1_grouped, P)
        group_weights(nc.scalar.copy, P + VECTOR_SHARE, P - VECTOR_SHARE, v2_w1_grouped, P + VECTOR_SHARE)
        quantize(w0_mx, w0_grouped)
        quantize(v2_w1, v2_w1_grouped)

        acc = [[psum.tile([P, HALF], F32, name=f"acc{i}{h}") for h in range(2)] for i in range(Q_TILES)]
        for i, (w_mx, w0) in enumerate(weights):
            multiply(acc[i][0][:], w_mx, w0, v01, HALF)
        for i, (w_mx, w0) in enumerate(weights):
            multiply(acc[i][1][:, :P], w_mx, w0, v2_w1, P)

        sigmoid_of_gate(0, GATE_HEAD, HALF)
        sigmoid_of_gate(0, HALF, DV)
        v3_grouped, v3 = og_tiles[0][:, :HALF].bitcast(BF16), mx_tiles("v3", P)
        group_values(turned_last, v3_grouped, 0)
        sigmoid_of_gate(1, 0, HALF)
        sigmoid_of_gate(1, HALF, DV)
        quantize(v3, v3_grouped)
        for i, (w_mx, w0) in enumerate(weights):
            multiply(acc[i][1][:, P:], w_mx, w0, v3, P)

        for h in range(2):
            cols = slice(h * HALF, (h + 1) * HALF)
            for i in range(Q_TILES):
                nc.vector.tensor_tensor(og_tiles[i][:, cols], acc[i][h][:], gate[:, i, cols], MULT)
                nc.sync.dma_start(out=out[0, i * P : (i + 1) * P, cols], in_=og_tiles[i][:, cols])
